import numpy as np
import ml_dtypes


def mxq(x, axis, fmt="e4m3"):
    dtype, down = {"e4m3": (ml_dtypes.float8_e4m3fn, 7), "e5m2": (ml_dtypes.float8_e5m2, 14)}[fmt]
    v = np.moveaxis(np.asarray(x, np.float32).astype(ml_dtypes.bfloat16).astype(np.float64), axis, -1)
    blocks = v.reshape(v.shape[:-1] + (-1, 32))
    amax = np.abs(blocks).max(-1, keepdims=True)
    byte = np.maximum(np.where(amax > 0, np.frexp(amax)[1] - 1 + 127, 0) - down, 1)
    scale = np.exp2(byte - 127.0)
    codes = (blocks / scale).astype(np.float32).astype(dtype).astype(np.float64)
    return np.moveaxis((codes * scale).reshape(v.shape), -1, axis)


WIDE = False


def mx_kscale(k):
    if not WIDE:
        return np.ones(k)
    levels = np.array([10, -10, 5, -5, 0])
    if k % 512:
        return np.exp2(np.random.permutation(np.resize(levels, k // 32))).repeat(32)
    a = np.empty((k // 512, 16))
    for p in range(k // 512):
        a[p, :8] = np.random.permutation(np.resize(levels, 8))
        for g in range(8):
            far = levels[np.abs(levels - a[p, g]) >= 10]
            a[p, g + 8] = far[np.random.randint(len(far))]
    return np.exp2(a.ravel()).repeat(32)


def f64(x):
    return np.asarray(x).astype(np.float64)


def striped(idx):
    return np.tile(idx.reshape(-1, 16).T, (8, 1)).astype(np.uint16)


def unstriped(offs):
    return offs[:16].T.reshape(-1).astype(np.int64)


E2M1 = np.array([0.0, 0.5, 1.0, 1.5, 2.0, 3.0, 4.0, 6.0, -0.0, -0.5, -1.0, -1.5, -2.0, -3.0, -4.0, -6.0])


def pack_weight(w, fmt):
    k, n = w.shape
    w = f64(np.asarray(w, np.float32).astype(ml_dtypes.bfloat16)).reshape(k // 32, 32, n)
    amax = np.abs(w).max(1)
    if fmt == "e4m3":
        byte = np.frexp(amax)[1] - 1 + 127 - 7
    else:
        mant, ex = np.frexp(amax / 6.0)
        byte = np.where(mant > 0.5, ex, ex - 1) + 127
    byte = np.clip(np.where(amax > 0, byte, 1), 1, 254)
    scaled = (w * np.exp2(127.0 - byte)[:, None, :]).reshape(k, n).astype(np.float32)
    by_word = np.ascontiguousarray(scaled.reshape(k // 512, 128, 4, n).transpose(0, 1, 3, 2))
    if fmt == "e4m3":
        words = by_word.astype(ml_dtypes.float8_e4m3fn).view(np.uint8)
    else:
        c = by_word.astype(ml_dtypes.float4_e2m1fn).view(np.uint8) & 0xF
        words = (c[..., 0::2] | (c[..., 1::2] << 4)).reshape(k // 512, 128, 2 * n)
    return np.ascontiguousarray(words), np.ascontiguousarray(byte.astype(np.uint8).reshape(k // 512, 16, n))


def unpack_weight(words, scales, fmt):
    g, _, n = scales.shape
    words = np.ascontiguousarray(words).reshape(g, 128, n, -1)
    if fmt == "e4m3":
        vals = words.view(ml_dtypes.float8_e4m3fn).astype(np.float64)
    else:
        nib = np.empty((g, 128, n, 4), np.uint8)
        nib[..., 0::2] = words & 0xF
        nib[..., 1::2] = words >> 4
        vals = E2M1[nib]
    vals = vals * np.repeat(np.exp2(scales.astype(np.float64) - 127.0), 8, axis=1)[..., None]
    return vals.transpose(0, 1, 3, 2).reshape(g * 512, n)


def pack_table(v):
    words, scales = pack_weight(v, "e4m3")
    return np.concatenate([words.reshape(words.shape[0], -1), scales.reshape(scales.shape[0], -1)], axis=1)


def unpack_table(tab):
    g, t = tab.shape[0], tab.shape[1] // 528
    return unpack_weight(tab[:, :512 * t].reshape(g, 128, t, 4), tab[:, 512 * t:].reshape(g, 16, t), "e4m3")


def gelu(v):
    return 0.5 * v * (1.0 + np.tanh(np.sqrt(2.0 / np.pi) * (v + 0.044715 * v**3)))


K, M, T, S = 2048, 128, 1024, 512


def setup_inputs():
    n = np.random.standard_normal
    s = mx_kscale(K)[:, None]
    s2 = mx_kscale(512)[:, None]
    p_w4 = pack_weight(n((K, M)) / np.sqrt(K) / s, "e2m1")
    return {
        "tab": pack_table(n((K, T)) * s),
        "w4_words": p_w4[0],
        "w4_scales": p_w4[1],
        "c": (n((512, S)) * s2).astype(np.float32),
        "u": (n((512, M)) / np.sqrt(512) / s2).astype(np.float32),
        "b": (0.3 * n(128)).astype(np.float32),
        "wgo": np.tile(np.random.uniform(0.5, 2.0, S), (128, 1)).astype(np.float32),
        "offs": striped(np.random.permutation(T)[:S]),
        "offs2": striped(np.random.permutation(T)[:S]),
    }


def reference(tab, w4_words, w4_scales, c, u, b, wgo, offs, offs2):
    tab_ = unpack_table(tab)[:, unstriped(offs)]
    w4_ = unpack_weight(w4_words, w4_scales, "e2m1")
    c_ = mxq(f64(c), 0, "e4m3")
    u_ = mxq(f64(u), 0, "e4m3")
    y = w4_.T @ tab_ + u_.T @ c_
    out = np.zeros((M, T))
    out[:, unstriped(offs2)] = f64(wgo)[0] * (gelu(y + f64(b)[:, None]))
    return out

@@ -1,0 +1,171 @@
+from contextlib import ExitStack
+
+import concourse.mybir as mybir
+from concourse.masks import make_identity
+
+K, M, T, S, L = 2048, 128, 1024, 512, 512
+FLOPS = 2 * (K + L) * M * S
+
+F32 = mybir.dt.float32
+BF16 = mybir.dt.bfloat16
+I32 = mybir.dt.int32
+U32 = mybir.dt.uint32
+U16 = mybir.dt.uint16
+U8 = mybir.dt.uint8
+FP8X4 = mybir.dt.float8_e4m3fn_x4
+FP4X4 = mybir.dt.float4_e2m1fn_x4
+GELU = mybir.ActivationFunctionType.Gelu_apprx_tanh
+MULT = mybir.AluOpType.mult
+
+P = 128
+PACK = 4
+PASSES = K // (P * PACK)
+QUADS = 4
+ROWS = 4
+N = 128
+HALF = S // 2
+PER_COL = 16
+
+
+def tile_list_tabscat_d_gelu_kernel(tc, tab, w4_words, w4_scales, c, u, b, wgo, offs, offs2, out):
+    nc = tc.nc
+    with ExitStack() as ctx:
+        keep = ctx.enter_context(tc.tile_pool(name="keep", bufs=1))
+        psum = ctx.enter_context(tc.psum_pool(name="psum", bufs=1))
+
+        def sb(name, shape, dtype, tag=None):
+            return keep.tile(shape, dtype, name=name, tag=tag or name, align_bytes=64)
+
+        pick = keep.tile([P, S // PER_COL], U16, name="pick")
+        place = keep.tile([P, S // PER_COL], U16, name="place")
+        tab_rows = sb("tab_rows", [P, T], U8)
+        got_rows = sb("got_rows", [P, S], U8)
+        both_rows = sb("both_rows", [P, S + M], U8)
+        planes = sb("planes", [P, PASSES, S + M], U8)
+        tab_words = {}
+        got_words = [sb(f"got_words{a}", [P, S], U32) for a in range(PASSES)]
+        w_words = sb("w_words", [P, PASSES, 2 * M], U8)
+        u_bf = sb("u_bf", [P, M, PACK], BF16)
+        u_codes = sb("u_codes", [P, M], U32)
+        u_scales = sb("u_scales", [P, M], U8)
+        c_raw = {}
+        c_bf = [sb(f"c_bf{q}", [P, N, PACK], BF16) for q in range(4)]
+        c_codes = {}
+        c_scales = [sb(f"c_scales{q}", [P, N], U8) for q in range(4)]
+        bias = sb("bias", [P, 1], F32)
+        gain = sb("gain", [P, S], F32)
+        gain_col = sb("gain_col", [P, PACK], F32)
+        ident = sb("ident", [P, P], F32)
+        gain_ps = psum.tile([P, PACK, P], F32, name="gain_ps")
+        act = {}
+        page = sb("page", [P, T], F32)
+        acc = [psum.tile([M, N], F32, name=f"acc{q}") for q in range(4)]
+
+        def load_words(a, tag=None):
+            tab_words[a] = sb(f"tab_words{a}", [P, T], I32, tag)
+            src = tab[a, 0 : P * PACK * T].rearrange("(p x) -> p x", p=P).bitcast(I32)
+            nc.sync.dma_start(out=tab_words[a][:], in_=src)
+
+        def load_c(q, tag):
+            c_raw[q] = sb(f"c_raw{q}", [P, PACK, N], F32, tag)
+            nc.sync.dma_start(out=c_raw[q][:], in_=c[:, q * N : (q + 1) * N].rearrange("(p j) w -> p j w", j=PACK))
+
+        def gather_words(a, lo, hi):
+            nc.vector.tensor_copy(
+                out=got_words[a][:, lo:hi],
+                in_=tab_words[a][:].bitcast(U32).indirect(pick[:, lo // PER_COL : hi // PER_COL]),
+            )
+
+        def weave_c(q):
+            nc.scalar.copy(out=c_bf[q][:], in_=c_raw[q][:].rearrange("p j w -> p w j"))
+
+        def quant_c(q):
+            c_codes[q] = sb(f"c_codes{q}", [P, N], U32)
+            nc.vector.quantize_mx(out=c_codes[q][:].bitcast(FP8X4), scales=c_scales[q][:], in_=c_bf[q][:].rearrange("p w j -> p (w j)"))
+
+        def tab_pass(a, q, start, stop):
+            cols = slice(q * N, (q + 1) * N)
+            nc.tensor.matmul_mx(
+                out=acc[q][:], lhsT=w_words[:, a, :].bitcast(FP4X4), lhsT_scale=planes[:, a, S : S + M],
+                rhs=got_words[a][:, cols].bitcast(FP8X4), rhs_scale=planes[:, a, cols], start=start, stop=stop,
+            )
+
+        def c_pass(q, stop):
+            nc.tensor.matmul_mx(
+                out=acc[q][:], lhsT=u_codes[:].bitcast(FP8X4), lhsT_scale=u_scales[:],
+                rhs=c_codes[q][:].bitcast(FP8X4), rhs_scale=c_scales[q][:], start=False, stop=stop,
+            )
+
+        def gelu(q):
+            act[q] = sb(f"act{q}", [P, N], F32)
+            nc.scalar.activation(out=act[q][:], in_=acc[q][:], func=GELU, bias=bias[:])
+
+        def scatter(q):
+            cols = slice(q * N, (q + 1) * N)
+            nc.vector.tensor_tensor(page[:].indirect(place[:, q * N // PER_COL : (q + 1) * N // PER_COL]), act[q][:], gain[:, cols], MULT)
+
+        nc.vector.memset(tab_rows[0:32, :].bitcast(I32), 0)
+        nc.vector.memset(tab_rows[96:128, :].bitcast(I32), 0)
+        nc.vector.memset(planes[:].rearrange("p a n -> p (a n)").bitcast(I32), 0)
+        make_identity(nc, ident[:])
+        nc.gpsimd.memset(page[:], 0.0)
+        warm = sb("warm", [P, 2], F32)
+        nc.vector.memset(warm[:, 0:1], 0.0)
+        nc.scalar.activation(out=warm[:, 1:2], in_=warm[:, 0:1], func=GELU)
+
+        nc.sync.dma_start(pick[:], offs)
+        nc.scalar.dma_start(
+            out=tab_rows[32:96, :].bitcast(I32),
+            in_=tab[:, P * PACK * T :].rearrange("a (q t) -> q a t", t=T).bitcast(I32),
+        )
+        nc.scalar.dma_start(
+            out=both_rows[32:96, S : S + M].bitcast(I32),
+            in_=w4_scales.rearrange("a q n -> q a n").bitcast(I32),
+        )
+        nc.scalar.dma_start(out=gain_col[:], in_=wgo[0, :].rearrange("(p t) -> p t", t=PACK))
+        load_words(0)
+        nc.sync.dma_start(place[:], offs2)
+        load_words(1)
+        nc.gpsimd.dma_start(out=bias[:], in_=b.rearrange("(p o) -> p o", o=1))
+        nc.sync.dma_start(out=w_words[:].bitcast(I32), in_=w4_words.rearrange("a p x -> p a x").bitcast(I32))
+        load_words(2)
+        for t in range(PACK):
+            nc.tensor.transpose(gain_ps[:, t, :], gain_col[:, t : t + 1].to_broadcast([P, P]), ident[:])
+        nc.scalar.copy(out=gain[:].rearrange("m (p t) -> m p t", t=PACK), in_=gain_ps[:].rearrange("m t p -> m p t"))
+
+        nc.vector.tensor_copy(out=got_rows[:], in_=tab_rows[:].indirect(pick[:]))
+        nc.vector.tensor_copy(out=both_rows[:, 0:S].bitcast(I32), in_=got_rows[:].bitcast(I32))
+        for g in range(QUADS):
+            nc.sync.dma_start(
+                out=planes[32 * g : 32 * g + ROWS].rearrange("r a s -> r (a s)").bitcast(I32),
+                in_=both_rows[32 + 16 * g : 32 + 16 * (g + 1), :].bitcast(I32),
+            )
+        load_c(0, "tab_rows")
+        u_raw = sb("u_raw", [P, PACK, M], F32, "got_rows")
+        nc.sync.dma_start(out=u_raw[:], in_=u.rearrange("(p j) n -> p j n", j=PACK))
+        gather_words(0, 0, S)
+        load_words(3, "tab_words0")
+        gather_words(1, 0, S)
+        load_c(1, "tab_words1")
+        weave_c(0)
+        load_c(2, "both_rows")
+        load_c(3, "tab_rows")
+        gather_words(2, 0, S)
+        quant_c(0)
+        nc.scalar.copy(out=u_bf[:], in_=u_raw[:].rearrange("p j n -> p n j"))
+        nc.vector.quantize_mx(out=u_codes[:].bitcast(FP8X4), scales=u_scales[:], in_=u_bf[:].rearrange("p n j -> p (n j)"))
+        gather_words(3, 0, N)
+        gather_words(3, N, S)
+        for q in range(4):
+            if q >= 1:
+                weave_c(q)
+                if q >= 2:
+                    scatter(q - 2)
+                quant_c(q)
+            for a in range(PASSES):
+                tab_pass(a, q, a == 0, False)
+            c_pass(q, True)
+            gelu(q)
+        scatter(2)
+        scatter(3)
+        nc.sync.dma_start(out=out, in_=page[:])

@@ -42,33 +42,31 @@ def tile_list_tabscat_d_gelu_kernel(tc, tab, w4_words, w4_scales, c, u, b, wgo, 
         got_rows = sb("got_rows", [P, S], U8)
         both_rows = sb("both_rows", [P, S + M], U8)
         planes = sb("planes", [P, PASSES, S + M], U8)
-        tab_words = {}
+        tab_words = []
         got_words = [sb(f"got_words{a}", [P, S], U32) for a in range(PASSES)]
         w_words = sb("w_words", [P, PASSES, 2 * M], U8)
+        u_raw = sb("u_raw", [P, PACK, M], F32)
         u_bf = sb("u_bf", [P, M, PACK], BF16)
         u_codes = sb("u_codes", [P, M], U32)
         u_scales = sb("u_scales", [P, M], U8)
-        c_raw = {}
-        c_bf = [sb(f"c_bf{q}", [P, N, PACK], BF16) for q in range(4)]
-        c_codes = {}
-        c_scales = [sb(f"c_scales{q}", [P, N], U8) for q in range(4)]
+        c_raw = sb("c_raw", [P, PACK, S - N], F32)
+        widths = [2 * N, N, N]
+        c_bf = [sb(f"c_bf{h}", [P, w, PACK], BF16) for h, w in enumerate(widths)]
+        c_codes = [sb(f"c_codes{h}", [P, w], U32) for h, w in enumerate(widths)]
+        c_scales = [sb(f"c_scales{h}", [P, w], U8) for h, w in enumerate(widths)]
         bias = sb("bias", [P, 1], F32)
         gain = sb("gain", [P, S], F32)
         gain_col = sb("gain_col", [P, PACK], F32)
         ident = sb("ident", [P, P], F32)
-        gain_ps = psum.tile([P, PACK, P], F32, name="gain_ps")
-        act = {}
+        act = sb("act", [P, S], F32)
         page = sb("page", [P, T], F32)
+        gain_ps = psum.tile([P, PACK, P], F32, name="gain_ps")
         acc = [psum.tile([M, N], F32, name=f"acc{q}") for q in range(4)]
 
         def load_words(a, tag=None):
-            tab_words[a] = sb(f"tab_words{a}", [P, T], I32, tag)
+            tab_words.append(sb(f"tab_words{a}", [P, T], I32, tag))
             src = tab[a, 0 : P * PACK * T].rearrange("(p x) -> p x", p=P).bitcast(I32)
             nc.sync.dma_start(out=tab_words[a][:], in_=src)
-
-        def load_c(q, tag):
-            c_raw[q] = sb(f"c_raw{q}", [P, PACK, N], F32, tag)
-            nc.sync.dma_start(out=c_raw[q][:], in_=c[:, q * N : (q + 1) * N].rearrange("(p j) w -> p j w", j=PACK))
 
         def gather_words(a, lo, hi):
             nc.vector.tensor_copy(
@@ -76,12 +74,11 @@ def tile_list_tabscat_d_gelu_kernel(tc, tab, w4_words, w4_scales, c, u, b, wgo, 
                 in_=tab_words[a][:].bitcast(U32).indirect(pick[:, lo // PER_COL : hi // PER_COL]),
             )
 
-        def weave_c(q):
-            nc.scalar.copy(out=c_bf[q][:], in_=c_raw[q][:].rearrange("p j w -> p w j"))
+        def weave(dst, src):
+            nc.scalar.copy(out=dst, in_=src.rearrange("p j w -> p w j"))
 
-        def quant_c(q):
-            c_codes[q] = sb(f"c_codes{q}", [P, N], U32)
-            nc.vector.quantize_mx(out=c_codes[q][:].bitcast(FP8X4), scales=c_scales[q][:], in_=c_bf[q][:].rearrange("p w j -> p (w j)"))
+        def quantise(codes, scales, woven):
+            nc.vector.quantize_mx(out=codes[:].bitcast(FP8X4), scales=scales[:], in_=woven[:].rearrange("p w j -> p (w j)"))
 
         def tab_pass(a, q, start, stop):
             cols = slice(q * N, (q + 1) * N)
@@ -90,30 +87,27 @@ def tile_list_tabscat_d_gelu_kernel(tc, tab, w4_words, w4_scales, c, u, b, wgo, 
                 rhs=got_words[a][:, cols].bitcast(FP8X4), rhs_scale=planes[:, a, cols], start=start, stop=stop,
             )
 
-        def c_pass(q, stop):
+        def c_pass(q, start, stop):
+            h = max(q - 1, 0)
+            cols = slice(q * N, (q + 1) * N) if h == 0 else slice(0, N)
             nc.tensor.matmul_mx(
                 out=acc[q][:], lhsT=u_codes[:].bitcast(FP8X4), lhsT_scale=u_scales[:],
-                rhs=c_codes[q][:].bitcast(FP8X4), rhs_scale=c_scales[q][:], start=False, stop=stop,
+                rhs=c_codes[h][:, cols].bitcast(FP8X4), rhs_scale=c_scales[h][:, cols], start=start, stop=stop,
             )
 
-        def gelu(q):
-            act[q] = sb(f"act{q}", [P, N], F32)
-            nc.scalar.activation(out=act[q][:], in_=acc[q][:], func=GELU, bias=bias[:])
-
-        def scatter(q):
-            cols = slice(q * N, (q + 1) * N)
-            nc.vector.tensor_tensor(page[:].indirect(place[:, q * N // PER_COL : (q + 1) * N // PER_COL]), act[q][:], gain[:, cols], MULT)
+        def scatter(lo, hi):
+            nc.vector.tensor_tensor(page[:].indirect(place[:, lo // PER_COL : hi // PER_COL]), act[:, lo:hi], gain[:, lo:hi], MULT)
 
         nc.vector.memset(tab_rows[0:32, :].bitcast(I32), 0)
         nc.vector.memset(tab_rows[96:128, :].bitcast(I32), 0)
         nc.vector.memset(planes[:].rearrange("p a n -> p (a n)").bitcast(I32), 0)
-        make_identity(nc, ident[:])
-        nc.gpsimd.memset(page[:], 0.0)
+        nc.vector.memset(page[:], 0.0)
         warm = sb("warm", [P, 2], F32)
         nc.vector.memset(warm[:, 0:1], 0.0)
         nc.scalar.activation(out=warm[:, 1:2], in_=warm[:, 0:1], func=GELU)
 
         nc.sync.dma_start(pick[:], offs)
+        load_words(0)
         nc.scalar.dma_start(
             out=tab_rows[32:96, :].bitcast(I32),
             in_=tab[:, P * PACK * T :].rearrange("a (q t) -> q a t", t=T).bitcast(I32),
@@ -122,50 +116,52 @@ def tile_list_tabscat_d_gelu_kernel(tc, tab, w4_words, w4_scales, c, u, b, wgo, 
             out=both_rows[32:96, S : S + M].bitcast(I32),
             in_=w4_scales.rearrange("a q n -> q a n").bitcast(I32),
         )
-        nc.scalar.dma_start(out=gain_col[:], in_=wgo[0, :].rearrange("(p t) -> p t", t=PACK))
-        load_words(0)
         nc.sync.dma_start(place[:], offs2)
-        load_words(1)
+        nc.scalar.dma_start(out=gain_col[:], in_=wgo[0, :].rearrange("(p t) -> p t", t=PACK))
         nc.gpsimd.dma_start(out=bias[:], in_=b.rearrange("(p o) -> p o", o=1))
+        make_identity(nc, ident[:])
+        nc.sync.dma_start(out=u_raw[:], in_=u.rearrange("(p j) n -> p j n", j=PACK))
+        nc.sync.dma_start(out=c_raw[:], in_=c[:, 0 : S - N].rearrange("(p j) w -> p j w", j=PACK))
         nc.sync.dma_start(out=w_words[:].bitcast(I32), in_=w4_words.rearrange("a p x -> p a x").bitcast(I32))
-        load_words(2)
-        for t in range(PACK):
-            nc.tensor.transpose(gain_ps[:, t, :], gain_col[:, t : t + 1].to_broadcast([P, P]), ident[:])
-        nc.scalar.copy(out=gain[:].rearrange("m (p t) -> m p t", t=PACK), in_=gain_ps[:].rearrange("m t p -> m p t"))
 
         nc.vector.tensor_copy(out=got_rows[:], in_=tab_rows[:].indirect(pick[:]))
+        load_words(1, "tab_rows")
         nc.vector.tensor_copy(out=both_rows[:, 0:S].bitcast(I32), in_=got_rows[:].bitcast(I32))
         for g in range(QUADS):
             nc.sync.dma_start(
                 out=planes[32 * g : 32 * g + ROWS].rearrange("r a s -> r (a s)").bitcast(I32),
                 in_=both_rows[32 + 16 * g : 32 + 16 * (g + 1), :].bitcast(I32),
             )
-        load_c(0, "tab_rows")
-        u_raw = sb("u_raw", [P, PACK, M], F32, "got_rows")
-        nc.sync.dma_start(out=u_raw[:], in_=u.rearrange("(p j) n -> p j n", j=PACK))
         gather_words(0, 0, S)
-        load_words(3, "tab_words0")
+        load_words(2, "tab_words0")
+        weave(u_bf[:], u_raw[:])
+        load_words(3, "u_raw")
+        quantise(u_codes, u_scales, u_bf)
+        c_last = sb("c_last", [P, PACK, N], F32, "u_bf")
+        nc.sync.dma_start(out=c_last[:], in_=c[:, S - N : S].rearrange("(p j) w -> p j w", j=PACK))
+        weave(c_bf[0][:], c_raw[:, :, 0 : 2 * N])
+        quantise(c_codes[0], c_scales[0], c_bf[0])
+        weave(c_bf[1][:], c_raw[:, :, 2 * N : 3 * N])
         gather_words(1, 0, S)
-        load_c(1, "tab_words1")
-        weave_c(0)
-        load_c(2, "both_rows")
-        load_c(3, "tab_rows")
+        quantise(c_codes[1], c_scales[1], c_bf[1])
         gather_words(2, 0, S)
-        quant_c(0)
-        nc.scalar.copy(out=u_bf[:], in_=u_raw[:].rearrange("p j n -> p n j"))
-        nc.vector.quantize_mx(out=u_codes[:].bitcast(FP8X4), scales=u_scales[:], in_=u_bf[:].rearrange("p n j -> p (n j)"))
         gather_words(3, 0, N)
         gather_words(3, N, S)
+        weave(c_bf[2][:], c_last[:])
+        quantise(c_codes[2], c_scales[2], c_bf[2])
+        for t in range(PACK):
+            nc.tensor.transpose(gain_ps[:, t, :], gain_col[:, t : t + 1].to_broadcast([P, P]), ident[:])
+        nc.scalar.copy(out=gain[:].rearrange("m (p t) -> m p t", t=PACK), in_=gain_ps[:].rearrange("m t p -> m p t"))
         for q in range(4):
-            if q >= 1:
-                weave_c(q)
-                if q >= 2:
-                    scatter(q - 2)
-                quant_c(q)
+            c_is_last = q == 3
+            if not c_is_last:
+                c_pass(q, True, False)
             for a in range(PASSES):
-                tab_pass(a, q, a == 0, False)
-            c_pass(q, True)
-            gelu(q)
-        scatter(2)
-        scatter(3)
+                tab_pass(a, q, c_is_last and a == 0, not c_is_last and a == PASSES - 1)
+            if c_is_last:
+                c_pass(q, False, True)
+            nc.scalar.activation(out=act[:, q * N : (q + 1) * N], in_=acc[q][:], func=GELU, bias=bias[:])
+        scatter(0, N)
+        scatter(N, S - N)
+        scatter(S - N, S)
         nc.sync.dma_start(out=out, in_=page[:])

@@ -23,7 +23,6 @@ PASSES = K // (P * PACK)
 QUADS = 4
 ROWS = 4
 N = 128
-HALF = S // 2
 PER_COL = 16
 
 
@@ -40,128 +39,140 @@ def tile_list_tabscat_d_gelu_kernel(tc, tab, w4_words, w4_scales, c, u, b, wgo, 
         place = keep.tile([P, S // PER_COL], U16, name="place")
         tab_rows = sb("tab_rows", [P, T], U8)
         got_rows = sb("got_rows", [P, S], U8)
-        both_rows = sb("both_rows", [P, S + M], U8)
-        planes = sb("planes", [P, PASSES, S + M], U8)
-        tab_words = []
+        got_scales = sb("got_scales", [P, PASSES, S], U8)
         got_words = [sb(f"got_words{a}", [P, S], U32) for a in range(PASSES)]
         w_words = sb("w_words", [P, PASSES, 2 * M], U8)
-        u_raw = sb("u_raw", [P, PACK, M], F32)
-        u_bf = sb("u_bf", [P, M, PACK], BF16)
-        u_codes = sb("u_codes", [P, M], U32)
-        u_scales = sb("u_scales", [P, M], U8)
-        c_raw = sb("c_raw", [P, PACK, S - N], F32)
-        widths = [2 * N, N, N]
-        c_bf = [sb(f"c_bf{h}", [P, w, PACK], BF16) for h, w in enumerate(widths)]
-        c_codes = [sb(f"c_codes{h}", [P, w], U32) for h, w in enumerate(widths)]
-        c_scales = [sb(f"c_scales{h}", [P, w], U8) for h, w in enumerate(widths)]
+        w_scales = sb("w_scales", [P, PASSES, M], U8)
         bias = sb("bias", [P, 1], F32)
         gain = sb("gain", [P, S], F32)
         gain_col = sb("gain_col", [P, PACK], F32)
         ident = sb("ident", [P, P], F32)
-        act = sb("act", [P, S], F32)
         page = sb("page", [P, T], F32)
         gain_ps = psum.tile([P, PACK, P], F32, name="gain_ps")
         acc = [psum.tile([M, N], F32, name=f"acc{q}") for q in range(4)]
 
         def load_words(a, tag=None):
-            tab_words.append(sb(f"tab_words{a}", [P, T], I32, tag))
-            src = tab[a, 0 : P * PACK * T].rearrange("(p x) -> p x", p=P).bitcast(I32)
-            nc.sync.dma_start(out=tab_words[a][:], in_=src)
+            words = sb(f"tab_words{a}", [P, T], I32, tag)
+            nc.sync.dma_start(out=words[:], in_=tab[a, 0 : P * PACK * T].rearrange("(p x) -> p x", p=P).bitcast(I32))
+            return words
 
-        def gather_words(a, lo, hi):
+        def load_rows(name, src, tag=None):
+            raw = sb(name, [P, PACK, src.shape[1]], F32, tag)
+            nc.sync.dma_start(out=raw[:], in_=src.rearrange("(p j) w -> p j w", j=PACK))
+            return raw
+
+        def gather_words(a, words, lo, hi):
             nc.vector.tensor_copy(
                 out=got_words[a][:, lo:hi],
-                in_=tab_words[a][:].bitcast(U32).indirect(pick[:, lo // PER_COL : hi // PER_COL]),
+                in_=words[:].bitcast(U32).indirect(pick[:, lo // PER_COL : hi // PER_COL]),
             )
 
-        def weave(dst, src):
-            nc.scalar.copy(out=dst, in_=src.rearrange("p j w -> p w j"))
+        def weave(dst, raw):
+            nc.scalar.copy(out=dst, in_=raw[:].rearrange("p j w -> p w j"))
 
-        def quantise(codes, scales, woven):
+        def quantise(name, woven):
+            width = woven.shape[1]
+            codes = sb(f"{name}_codes", [P, width], U32)
+            scales = sb(f"{name}_scales", [P, width], U8)
             nc.vector.quantize_mx(out=codes[:].bitcast(FP8X4), scales=scales[:], in_=woven[:].rearrange("p w j -> p (w j)"))
+            return [(codes[:, i : i + N].bitcast(FP8X4), scales[:, i : i + N]) for i in range(0, width, N)]
 
-        def tab_pass(a, q, start, stop):
+        def tab_pass(a, q, stop=False):
             cols = slice(q * N, (q + 1) * N)
             nc.tensor.matmul_mx(
-                out=acc[q][:], lhsT=w_words[:, a, :].bitcast(FP4X4), lhsT_scale=planes[:, a, S : S + M],
-                rhs=got_words[a][:, cols].bitcast(FP8X4), rhs_scale=planes[:, a, cols], start=start, stop=stop,
+                out=acc[q][:], lhsT=w_words[:, a, :].bitcast(FP4X4), lhsT_scale=w_scales[:, a, :],
+                rhs=got_words[a][:, cols].bitcast(FP8X4), rhs_scale=got_scales[:, a, cols], start=a == 0, stop=stop,
             )
 
-        def c_pass(q, start, stop):
-            h = max(q - 1, 0)
-            cols = slice(q * N, (q + 1) * N) if h == 0 else slice(0, N)
+        def c_pass(q, u_mx, c_mx, stop):
             nc.tensor.matmul_mx(
-                out=acc[q][:], lhsT=u_codes[:].bitcast(FP8X4), lhsT_scale=u_scales[:],
-                rhs=c_codes[h][:, cols].bitcast(FP8X4), rhs_scale=c_scales[h][:, cols], start=start, stop=stop,
+                out=acc[q][:], lhsT=u_mx[0], lhsT_scale=u_mx[1], rhs=c_mx[0], rhs_scale=c_mx[1], start=False, stop=stop,
             )
 
-        def scatter(lo, hi):
-            nc.vector.tensor_tensor(page[:].indirect(place[:, lo // PER_COL : hi // PER_COL]), act[:, lo:hi], gain[:, lo:hi], MULT)
+        def gelu(q, dst):
+            nc.scalar.activation(out=dst, in_=acc[q][:], func=GELU, bias=bias[:])
 
+        def scatter(lo, hi, act):
+            nc.vector.tensor_tensor(page[:].indirect(place[:, lo // PER_COL : hi // PER_COL]), act[:], gain[:, lo:hi], MULT)
+
+        nc.vector.memset(w_scales[:].rearrange("p a n -> p (a n)").bitcast(I32), 0)
         nc.vector.memset(tab_rows[0:32, :].bitcast(I32), 0)
         nc.vector.memset(tab_rows[96:128, :].bitcast(I32), 0)
-        nc.vector.memset(planes[:].rearrange("p a n -> p (a n)").bitcast(I32), 0)
+        nc.vector.memset(got_scales[:].rearrange("p a n -> p (a n)").bitcast(I32), 0)
         nc.vector.memset(page[:], 0.0)
         warm = sb("warm", [P, 2], F32)
         nc.vector.memset(warm[:, 0:1], 0.0)
         nc.scalar.activation(out=warm[:, 1:2], in_=warm[:, 0:1], func=GELU)
 
         nc.sync.dma_start(pick[:], offs)
-        load_words(0)
         nc.scalar.dma_start(
             out=tab_rows[32:96, :].bitcast(I32),
             in_=tab[:, P * PACK * T :].rearrange("a (q t) -> q a t", t=T).bitcast(I32),
         )
-        nc.scalar.dma_start(
-            out=both_rows[32:96, S : S + M].bitcast(I32),
-            in_=w4_scales.rearrange("a q n -> q a n").bitcast(I32),
-        )
-        nc.sync.dma_start(place[:], offs2)
         nc.scalar.dma_start(out=gain_col[:], in_=wgo[0, :].rearrange("(p t) -> p t", t=PACK))
-        nc.gpsimd.dma_start(out=bias[:], in_=b.rearrange("(p o) -> p o", o=1))
-        make_identity(nc, ident[:])
-        nc.sync.dma_start(out=u_raw[:], in_=u.rearrange("(p j) n -> p j n", j=PACK))
-        nc.sync.dma_start(out=c_raw[:], in_=c[:, 0 : S - N].rearrange("(p j) w -> p j w", j=PACK))
+        nc.scalar.dma_start(out=bias[:], in_=b.rearrange("(p o) -> p o", o=1))
+        words0 = load_words(0)
+        nc.sync.dma_start(place[:], offs2)
+        words1 = load_words(1)
+        u_raw = load_rows("u_raw", u)
         nc.sync.dma_start(out=w_words[:].bitcast(I32), in_=w4_words.rearrange("a p x -> p a x").bitcast(I32))
-
-        nc.vector.tensor_copy(out=got_rows[:], in_=tab_rows[:].indirect(pick[:]))
-        load_words(1, "tab_rows")
-        nc.vector.tensor_copy(out=both_rows[:, 0:S].bitcast(I32), in_=got_rows[:].bitcast(I32))
+        words2 = load_words(2)
+        make_identity(nc, ident[:])
         for g in range(QUADS):
-            nc.sync.dma_start(
-                out=planes[32 * g : 32 * g + ROWS].rearrange("r a s -> r (a s)").bitcast(I32),
-                in_=both_rows[32 + 16 * g : 32 + 16 * (g + 1), :].bitcast(I32),
+            nc.gpsimd.dma_start(
+                out=w_scales[32 * g : 32 * g + ROWS].bitcast(I32),
+                in_=w4_scales[:, ROWS * g : ROWS * (g + 1), :].rearrange("a r n -> r a n").bitcast(I32),
             )
-        gather_words(0, 0, S)
-        load_words(2, "tab_words0")
-        weave(u_bf[:], u_raw[:])
-        load_words(3, "u_raw")
-        quantise(u_codes, u_scales, u_bf)
-        c_last = sb("c_last", [P, PACK, N], F32, "u_bf")
-        nc.sync.dma_start(out=c_last[:], in_=c[:, S - N : S].rearrange("(p j) w -> p j w", j=PACK))
-        weave(c_bf[0][:], c_raw[:, :, 0 : 2 * N])
-        quantise(c_codes[0], c_scales[0], c_bf[0])
-        weave(c_bf[1][:], c_raw[:, :, 2 * N : 3 * N])
-        gather_words(1, 0, S)
-        quantise(c_codes[1], c_scales[1], c_bf[1])
-        gather_words(2, 0, S)
-        gather_words(3, 0, N)
-        gather_words(3, N, S)
-        weave(c_bf[2][:], c_last[:])
-        quantise(c_codes[2], c_scales[2], c_bf[2])
         for t in range(PACK):
             nc.tensor.transpose(gain_ps[:, t, :], gain_col[:, t : t + 1].to_broadcast([P, P]), ident[:])
         nc.scalar.copy(out=gain[:].rearrange("m (p t) -> m p t", t=PACK), in_=gain_ps[:].rearrange("m t p -> m p t"))
-        for q in range(4):
-            c_is_last = q == 3
-            if not c_is_last:
-                c_pass(q, True, False)
+
+        nc.vector.tensor_copy(out=got_rows[:], in_=tab_rows[:].indirect(pick[:]))
+        for g in range(QUADS):
+            nc.sync.dma_start(
+                out=got_scales[32 * g : 32 * g + ROWS].rearrange("r a s -> r (a s)").bitcast(I32),
+                in_=got_rows[32 + 16 * g : 32 + 16 * (g + 1), :].bitcast(I32),
+            )
+        c0_raw = load_rows("c0_raw", c[:, 0:N], "tab_rows")
+        gather_words(0, words0, 0, S)
+        words3 = load_words(3, "tab_words0")
+        uc0_bf = sb("uc0_bf", [P, M + N, PACK], BF16)
+        weave(uc0_bf[:, 0:M, :], u_raw)
+        c1_raw = load_rows("c1_raw", c[:, N : 2 * N], "u_raw")
+        c23_raw = load_rows("c23_raw", c[:, 2 * N : S], "got_rows")
+        gather_words(1, words1, 0, S)
+        weave(uc0_bf[:, M : M + N, :], c0_raw)
+        gather_words(2, words2, 0, S)
+        u_mx, c0_mx = quantise("uc0", uc0_bf)
+        gather_words(3, words3, 0, N)
+        for a in range(PASSES - 1):
+            tab_pass(a, 0)
+        c_pass(0, u_mx, c0_mx, False)
+        tab_pass(PASSES - 1, 0, True)
+        gather_words(3, words3, N, S)
+
+        c1_bf = sb("c1_bf", [P, N, PACK], BF16)
+        weave(c1_bf[:], c1_raw)
+        (c1_mx,) = quantise("c1", c1_bf)
+        act0 = sb("act0", [P, N], F32, "u_raw")
+        gelu(0, act0[:])
+        for a in range(PASSES):
+            tab_pass(a, 1)
+        c_pass(1, u_mx, c1_mx, True)
+        scatter(0, N, act0)
+
+        c23_bf = sb("c23_bf", [P, 2 * N, PACK], BF16)
+        weave(c23_bf[:], c23_raw)
+        c23_mx = quantise("c23", c23_bf)
+        act1 = sb("act1", [P, N], F32, "got_rows")
+        gelu(1, act1[:])
+        scatter(N, 2 * N, act1)
+
+        act23 = sb("act23", [P, 2 * N], F32)
+        for i, q in enumerate((2, 3)):
             for a in range(PASSES):
-                tab_pass(a, q, c_is_last and a == 0, not c_is_last and a == PASSES - 1)
-            if c_is_last:
-                c_pass(q, False, True)
-            nc.scalar.activation(out=act[:, q * N : (q + 1) * N], in_=acc[q][:], func=GELU, bias=bias[:])
-        scatter(0, N)
-        scatter(N, S - N)
-        scatter(S - N, S)
+                tab_pass(a, q)
+            c_pass(q, u_mx, c23_mx[i], True)
+            gelu(q, act23[:, i * N : (i + 1) * N])
+        scatter(2 * N, S, act23)
         nc.sync.dma_start(out=out, in_=page[:])

@@ -68,7 +68,7 @@ def tile_list_tabscat_d_gelu_kernel(tc, tab, w4_words, w4_scales, c, u, b, wgo, 
             )
 
         def weave(dst, raw):
-            nc.scalar.copy(out=dst, in_=raw[:].rearrange("p j w -> p w j"))
+            nc.scalar.copy(out=dst.rearrange("p (g i) j -> p g j i", i=4), in_=raw[:].rearrange("p j (g i) -> p g j i", i=4))
 
         def quantise(name, woven):
             width = woven.shape[1]

from contextlib import ExitStack

import concourse.mybir as mybir
from concourse.masks import make_identity

K, M, T, S, L = 2048, 128, 1024, 512, 512
FLOPS = 2 * (K + L) * M * S

F32 = mybir.dt.float32
BF16 = mybir.dt.bfloat16
I32 = mybir.dt.int32
U32 = mybir.dt.uint32
U16 = mybir.dt.uint16
U8 = mybir.dt.uint8
FP8X4 = mybir.dt.float8_e4m3fn_x4
FP4X4 = mybir.dt.float4_e2m1fn_x4
GELU = mybir.ActivationFunctionType.Gelu_apprx_tanh
MULT = mybir.AluOpType.mult

P = 128
PACK = 4
PASSES = K // (P * PACK)
QUADS = 4
ROWS = 4
N = 128
PER_COL = 16


def tile_list_tabscat_d_gelu_kernel(tc, tab, w4_words, w4_scales, c, u, b, wgo, offs, offs2, out):
    nc = tc.nc
    with ExitStack() as ctx:
        keep = ctx.enter_context(tc.tile_pool(name="keep", bufs=1))
        psum = ctx.enter_context(tc.psum_pool(name="psum", bufs=1))

        def sb(name, shape, dtype, tag=None):
            return keep.tile(shape, dtype, name=name, tag=tag or name, align_bytes=64)

        pick = keep.tile([P, S // PER_COL], U16, name="pick")
        place = keep.tile([P, S // PER_COL], U16, name="place")
        tab_rows = sb("tab_rows", [P, T], U8)
        got_rows = sb("got_rows", [P, S], U8)
        got_scales = sb("got_scales", [P, PASSES, S], U8)
        got_words = [sb(f"got_words{a}", [P, S], U32) for a in range(PASSES)]
        w_words = sb("w_words", [P, PASSES, 2 * M], U8)
        w_scales = sb("w_scales", [P, PASSES, M], U8)
        bias = sb("bias", [P, 1], F32)
        gain = sb("gain", [P, S], F32)
        gain_col = sb("gain_col", [P, PACK], F32)
        ident = sb("ident", [P, P], F32)
        page = sb("page", [P, T], F32)
        gain_ps = psum.tile([P, PACK, P], F32, name="gain_ps")
        acc = [psum.tile([M, N], F32, name=f"acc{q}") for q in range(4)]

        def load_words(a, tag=None):
            words = sb(f"tab_words{a}", [P, T], I32, tag)
            nc.sync.dma_start(out=words[:], in_=tab[a, 0 : P * PACK * T].rearrange("(p x) -> p x", p=P).bitcast(I32))
            return words

        def load_rows(name, src, tag=None):
            raw = sb(name, [P, PACK, src.shape[1]], F32, tag)
            nc.sync.dma_start(out=raw[:], in_=src.rearrange("(p j) w -> p j w", j=PACK))
            return raw

        def gather_words(a, words, lo, hi):
            nc.vector.tensor_copy(
                out=got_words[a][:, lo:hi],
                in_=words[:].bitcast(U32).indirect(pick[:, lo // PER_COL : hi // PER_COL]),
            )

        def weave(dst, raw):
            nc.scalar.copy(out=dst.rearrange("p (g i) j -> p g j i", i=4), in_=raw[:].rearrange("p j (g i) -> p g j i", i=4))

        def quantise(name, woven):
            width = woven.shape[1]
            codes = sb(f"{name}_codes", [P, width], U32)
            scales = sb(f"{name}_scales", [P, width], U8)
            nc.vector.quantize_mx(out=codes[:].bitcast(FP8X4), scales=scales[:], in_=woven[:].rearrange("p w j -> p (w j)"))
            return [(codes[:, i : i + N].bitcast(FP8X4), scales[:, i : i + N]) for i in range(0, width, N)]

        def tab_pass(a, q, stop=False):
            cols = slice(q * N, (q + 1) * N)
            nc.tensor.matmul_mx(
                out=acc[q][:], lhsT=w_words[:, a, :].bitcast(FP4X4), lhsT_scale=w_scales[:, a, :],
                rhs=got_words[a][:, cols].bitcast(FP8X4), rhs_scale=got_scales[:, a, cols], start=a == 0, stop=stop,
            )

        def c_pass(q, u_mx, c_mx, stop):
            nc.tensor.matmul_mx(
                out=acc[q][:], lhsT=u_mx[0], lhsT_scale=u_mx[1], rhs=c_mx[0], rhs_scale=c_mx[1], start=False, stop=stop,
            )

        def gelu(q, dst):
            nc.scalar.activation(out=dst, in_=acc[q][:], func=GELU, bias=bias[:])

        def scatter(lo, hi, act):
            nc.vector.tensor_tensor(page[:].indirect(place[:, lo // PER_COL : hi // PER_COL]), act[:], gain[:, lo:hi], MULT)

        nc.vector.memset(w_scales[:].rearrange("p a n -> p (a n)").bitcast(I32), 0)
        nc.vector.memset(tab_rows[0:32, :].bitcast(I32), 0)
        nc.vector.memset(tab_rows[96:128, :].bitcast(I32), 0)
        nc.vector.memset(got_scales[:].rearrange("p a n -> p (a n)").bitcast(I32), 0)
        nc.vector.memset(page[:], 0.0)
        warm = sb("warm", [P, 2], F32)
        nc.vector.memset(warm[:, 0:1], 0.0)
        nc.scalar.activation(out=warm[:, 1:2], in_=warm[:, 0:1], func=GELU)

        nc.sync.dma_start(pick[:], offs)
        nc.scalar.dma_start(
            out=tab_rows[32:96, :].bitcast(I32),
            in_=tab[:, P * PACK * T :].rearrange("a (q t) -> q a t", t=T).bitcast(I32),
        )
        nc.scalar.dma_start(out=gain_col[:], in_=wgo[0, :].rearrange("(p t) -> p t", t=PACK))
        nc.scalar.dma_start(out=bias[:], in_=b.rearrange("(p o) -> p o", o=1))
        words0 = load_words(0)
        nc.sync.dma_start(place[:], offs2)
        words1 = load_words(1)
        u_raw = load_rows("u_raw", u)
        nc.sync.dma_start(out=w_words[:].bitcast(I32), in_=w4_words.rearrange("a p x -> p a x").bitcast(I32))
        words2 = load_words(2)
        make_identity(nc, ident[:])
        for g in range(QUADS):
            nc.gpsimd.dma_start(
                out=w_scales[32 * g : 32 * g + ROWS].bitcast(I32),
                in_=w4_scales[:, ROWS * g : ROWS * (g + 1), :].rearrange("a r n -> r a n").bitcast(I32),
            )
        for t in range(PACK):
            nc.tensor.transpose(gain_ps[:, t, :], gain_col[:, t : t + 1].to_broadcast([P, P]), ident[:])
        nc.scalar.copy(out=gain[:].rearrange("m (p t) -> m p t", t=PACK), in_=gain_ps[:].rearrange("m t p -> m p t"))

        nc.vector.tensor_copy(out=got_rows[:], in_=tab_rows[:].indirect(pick[:]))
        for g in range(QUADS):
            nc.sync.dma_start(
                out=got_scales[32 * g : 32 * g + ROWS].rearrange("r a s -> r (a s)").bitcast(I32),
                in_=got_rows[32 + 16 * g : 32 + 16 * (g + 1), :].bitcast(I32),
            )
        c0_raw = load_rows("c0_raw", c[:, 0:N], "tab_rows")
        gather_words(0, words0, 0, S)
        words3 = load_words(3, "tab_words0")
        uc0_bf = sb("uc0_bf", [P, M + N, PACK], BF16)
        weave(uc0_bf[:, 0:M, :], u_raw)
        c1_raw = load_rows("c1_raw", c[:, N : 2 * N], "u_raw")
        c23_raw = load_rows("c23_raw", c[:, 2 * N : S], "got_rows")
        gather_words(1, words1, 0, S)
        weave(uc0_bf[:, M : M + N, :], c0_raw)
        gather_words(2, words2, 0, S)
        u_mx, c0_mx = quantise("uc0", uc0_bf)
        gather_words(3, words3, 0, N)
        for a in range(PASSES - 1):
            tab_pass(a, 0)
        c_pass(0, u_mx, c0_mx, False)
        tab_pass(PASSES - 1, 0, True)
        gather_words(3, words3, N, S)

        c1_bf = sb("c1_bf", [P, N, PACK], BF16)
        weave(c1_bf[:], c1_raw)
        (c1_mx,) = quantise("c1", c1_bf)
        act0 = sb("act0", [P, N], F32, "u_raw")
        gelu(0, act0[:])
        for a in range(PASSES):
            tab_pass(a, 1)
        c_pass(1, u_mx, c1_mx, True)
        scatter(0, N, act0)

        c23_bf = sb("c23_bf", [P, 2 * N, PACK], BF16)
        weave(c23_bf[:], c23_raw)
        c23_mx = quantise("c23", c23_bf)
        act1 = sb("act1", [P, N], F32, "got_rows")
        gelu(1, act1[:])
        scatter(N, 2 * N, act1)

        act23 = sb("act23", [P, 2 * N], F32)
        for i, q in enumerate((2, 3)):
            for a in range(PASSES):
                tab_pass(a, q)
            c_pass(q, u_mx, c23_mx[i], True)
            gelu(q, act23[:, i * N : (i + 1) * N])
        scatter(2 * N, S, act23)
        nc.sync.dma_start(out=out, in_=page[:])
